import numpy as np, ml_dtypes
CORES = [83,85,87,115,117,119]
N = 6
import mx_ref
BF = ml_dtypes.bfloat16
def entries(a):
    return np.ascontiguousarray(a.T).reshape(-1)
def table(e):
    return np.ascontiguousarray(np.reshape(e, (-1, 16)).T).astype(np.int32)
def gpick(z, e):
    return np.concatenate([z[16 * g:16 * g + 16][:, e[g]] for g in range(8)])
def tile(rs):
    return np.stack(rs, axis=2).reshape(128, -1).astype(BF)
def cut(t, i, w=512):
    return t[:, w * i:w * i + w]
def f(rng, *shape):
    return mx_ref.flush((rng.standard_normal(shape, dtype=np.float32) * np.exp2(rng.integers(-2, 3, shape[:-1] + (1,)))).astype(BF))
def wide(rng, *shape, cols=0):
    v = rng.standard_normal(shape, dtype=np.float32) * np.exp2(rng.integers(-12, 13, shape)).astype(np.float32)
    if cols: v *= np.repeat(np.exp2(rng.integers(-cols, cols + 1, shape[:-2] + (1, shape[-1] // 4))) * (rng.random(shape[:-2] + (1, shape[-1] // 4)) > 0.0625), 4, axis=-1).astype(np.float32)
    return mx_ref.flush(v.astype(BF))
TQ, O = 256, 1
def lay(k, q):
    return {"kp": np.repeat(k, 16, axis=1).astype(np.int32), "qp": np.stack([table(e) for e in q])}
def setup_inputs(rng):
    d = {"qx": f(rng, N, 128, 4 * TQ), "ky": f(rng, N, 128, 2048), "rt": np.repeat(f(rng, 1, 128, 1024), N, axis=0), "vv": f(rng, N, 128, 512 * O)}
    a = rng.integers(0, 3585)
    k = a + rng.integers(0, 512, (N, 8, 4))
    q = np.where(rng.random((N, TQ)) < 0.25, rng.integers(0, 4096, (N, TQ)), a + rng.integers(0, 512, (N, TQ)))
    return {**d, **lay(k, q)}
def setup_inputs_far(rng):
    d = setup_inputs(rng)
    k = rng.integers(1500, 2501, (N, 32)); q = np.zeros((N, TQ), int); a = int(rng.integers(0, 2))
    for r in range(N):
        k[r, rng.permutation(32)[:2]] = [1500, 2500]
        lo, hi = (2628, 4095) if (r + a) % 2 else (0, 1371)
        q[r] = rng.integers(lo, hi + 1, TQ)
        q[r, rng.permutation(TQ)[:2]] = [lo, hi]
    return {**d, **lay(k.reshape(N, 8, 4), q)}
def setup_inputs_same(rng):
    d = setup_inputs(rng); a = int(rng.integers(0, 4096))
    return {**d, **lay(np.full((N, 8, 4), a), np.full((N, TQ), a))}
def setup_inputs_descending(rng):
    d = setup_inputs(rng); a = rng.integers(0, 3585)
    q = np.stack([a + np.sort(rng.permutation(512)[:TQ])[::-1] for r in range(N)])
    k = np.stack([a + 16 * rng.permutation(32) + rng.integers(0, 16, 32) for r in range(N)])
    return {**d, **lay(k.reshape(N, 8, 4), q)}
def setup_inputs_near(rng):
    d = setup_inputs(rng); a = rng.integers(2049, 3968)
    q = np.stack([a + rng.permutation(TQ) % 128 for r in range(N)])
    k = np.stack([a + rng.permutation(np.concatenate([[0, 128], 1 + rng.permutation(127)[:30]])) for r in range(N)])
    return {**d, **lay(k.reshape(N, 8, 4), q)}
def setup_inputs_spread(rng):
    d = setup_inputs(rng); d["qx"] = wide(rng, N, 128, 4 * TQ, cols=4); return d
def check_inputs(d):
    b = []
    for r in range(N):
        k, q = d["kp"][r], entries(d["qp"][r])
        if d["rt"][r].tobytes() != d["rt"][0].tobytes(): b.append("rt")
        if k.min() < 0 or k.max() > 4095 or (k != np.repeat(k[::16], 16, axis=0)).any(): b.append("kp")
        if q.min() < 0 or q.max() > 4095: b.append("qp")
    return b
def reference(qx, ky, rt, vv, kp, qp):
    y = np.zeros((N, 128, O * TQ), np.float32)
    X = [mx_ref.quantize(qx[r]) for r in range(N)]
    for s in range(N):
        K = [mx_ref.quantize(np.ascontiguousarray(cut(ky[s], b))) for b in range(4)]
        V = [mx_ref.quantize(np.ascontiguousarray(cut(vv[s], o))) for o in range(O)]
        R = mx_ref.quantize(rt[s])
        P = [mx_ref.matmul(K[b], R) for b in range(4)]
        for r in range(N):
            A = []
            for b in range(4):
                c = np.clip(entries(qp[r])[None, :] - kp[s][::16, b][:, None], -128, 127) + 128
                A.append(np.maximum(mx_ref.matmul(K[b], X[r]) + gpick(P[b], c), np.float32(0)) * np.float32(0.03125))
            A = mx_ref.quantize(tile(A))
            for o in range(O): y[r][:, TQ * o:TQ * o + TQ] += mx_ref.matmul(V[o], A)
    return {"y": y}

@@ -1,0 +1,239 @@
+from concourse.bass import DstId, RemoteDMATransfer
+from concourse.mybir import dt, AluOpType, ActivationFunctionType
+
+NR, TQ, KV = 6, 256, 640
+F8 = "float8_e4m3fn_x4"
+SCRATCH = {
+    "kt": ("sbuf", [128, 2048], "bfloat16"),
+    "mt": ("sbuf", [128, 2048], "bfloat16"),
+    "vt": ("sbuf", [128, 512], "bfloat16"),
+    "mc": ("sbuf", [128, 512], F8), "mp": ("sbuf", [128, 512], "uint8"),
+    "qpi": ("sbuf", [128, 16], "int32"),
+    "ys": ("sbuf", [128, 256], "float32"),
+}
+for _i in range(4):
+    SCRATCH["pw%d" % _i] = ("sbuf", [128, 1024], "float32")
+    SCRATCH["gg%d" % _i] = ("sbuf", [128, 1024], "float32")
+    SCRATCH["ht%d" % _i] = ("sbuf", [128, 1024], "bfloat16")
+    SCRATCH["kf%d" % _i] = ("sbuf", [128, 4], "float32")
+    SCRATCH["ot%d" % _i] = ("sbuf", [128, 64], "float32")
+    SCRATCH["of%d" % _i] = ("sbuf", [128, 64], "uint16")
+for _i in range(NR):
+    SCRATCH["kvc%d" % _i] = ("sbuf", [128, KV], F8)
+    SCRATCH["kvp%d" % _i] = ("sbuf", [128, KV], "uint8")
+    SCRATCH["ac%d" % _i] = ("sbuf", [128, TQ], F8)
+    SCRATCH["ap%d" % _i] = ("sbuf", [128, TQ], "uint8")
+    SCRATCH["kpi%d" % _i] = ("sbuf", [128, 4], "int32")
+for _i in range(8):
+    SCRATCH["ps%d" % _i] = ("psum", [128, 512], "float32")
+
+SEMAPHORES = (["l_p", "l_q", "l_k", "l_v", "l_m", "vs", "ss", "ts", "sent", "stored", "q_in", "m_in"]
+              + ["%s_in%d" % (n, i) for n in ("p", "k", "v", "a") for i in range(NR)])
+
+
+def layout(T, topo):
+    cores = list(T.cores)
+    side = [[q for q in range(NR) if topo.chip(cores[q]) == topo.chip(cores[r])] for r in range(NR)]
+    local, mirror, worker = [], [], []
+    for r in range(NR):
+        i = side[r].index(r)
+        local.append(side[r][i:] + side[r][:i])
+        mirror.append([q for q in range(NR) if q not in side[r]][i])
+    for r in range(NR):
+        idle = [c for c in topo.cores_of(cores[r]) if c not in cores and c not in worker]
+        idle.sort(key=lambda c: (topo.die(c) != topo.die(cores[mirror[r]]), -c))
+        worker.append(idle[0])
+    return cores, local, mirror, worker
+
+
+def rank_program(g, core, T, topo):
+    cores, local, mirror, worker = layout(T, topo)
+    rank = T.rank_of(core)
+    if rank is None and core not in worker:
+        return
+    ADD, MAX, MIN, MULT, SUB = AluOpType.add, AluOpType.max, AluOpType.min, AluOpType.mult, AluOpType.subtract
+    COPY = ActivationFunctionType.Copy
+    eng = {"g": g, "v": g.vector, "s": g.scalar, "t": g.tensor}
+    done, seen, sent = {"v": 0, "s": 0, "t": 0}, {}, [0]
+
+    def after(q, *deps):
+        for d in deps:
+            sem = d[0] + "s" if d[0] in done else d[0]
+            if seen.get((q, sem), 0) < d[1]:
+                eng[q].wait_ge(T.sem[sem], d[1])
+                seen[(q, sem)] = d[1]
+
+    def mark(q, ins):
+        ins.then_inc(T.sem[q + "s"], 1)
+        done[q] += 1
+        return (q, done[q])
+
+    far = cores[mirror[0]] if topo.chip(core) == topo.chip(cores[0]) else cores[0]
+    near = [c for c in topo.cores_of(core) if c != core][0]
+    ALL = topo.engines(core, near)
+    OFF = topo.engines(core, far)
+    ON = [e for e in ALL if e not in OFF]
+    nALL, nOFF, nON = len(ALL), len(OFF), len(ON)
+
+    def ids(dsts):
+        out = []
+        for d in dsts:
+            rid, pid = topo.addr(d)[:2]
+            out.append(DstId(rid=rid, pnc=pid))
+        return out
+
+    def send(trs):
+        g.remote_dma_fused([RemoteDMATransfer(dst_ids=ids(ds), dma_engine_mask=sum(1 << e for e in es), remote_sem=T.sem[sem],
+                                              srcs=[src], dsts=[src] * len(ds)) for es, sem, src, ds in trs], local_sem=T.sem.sent)
+        sent[0] += sum(len(es) for es, _, _, _ in trs)
+
+    def cut(name, kind, a, b):
+        n = name[:-1] + kind + name[-1]
+        return T[n][:, a:b].bitcast(dt.uint8) if kind == "c" else T[n][:, a:b]
+
+    def ship(es, sem, name, a, b, ds):
+        for kind in "cp":
+            send([(es, sem, cut(name, kind, a, b), ds)])
+
+    def quantise(name, a, b, src, *deps):
+        after("v", *deps)
+        return mark("v", g.vector.quantize_mx(T[name[:-1] + "c" + name[-1]][:, a:b], T[name[:-1] + "p" + name[-1]][:, a:b], src))
+
+    banks = 7 if rank is not None else 8
+    drained, turn = [()] * 8, [0]
+
+    def lists(i, s, *deps):
+        after("v", *deps)
+        kf = T["kf%d" % i]
+        m = mark("v", g.vector.tensor_scalar(kf[:], T["kpi%d" % s][:], 128.0, None, SUB))
+        after("v", m)
+        for b in range(4):
+            m = mark("v", g.vector.tensor_scalar(T["ot%d" % i][:, 16 * b:16 * b + 16], T.qpi[:], kf[:, b:b + 1], 0.0, SUB, MAX))
+        after("v", m)
+        return mark("v", g.vector.tensor_scalar(T["of%d" % i][:], T["ot%d" % i][:], 255.0, None, MIN))
+
+    def products(s, *deps):
+        out = []
+        for b in range(4):
+            k = turn[0] % banks
+            turn[0] += 1
+            after("t", *drained[k], *deps)
+            m = mark("t", g.tensor.matmul_mx(T["ps%d" % k][:], T["kvc%d" % s][:, 128 * b:128 * b + 128], T["kvp%d" % s][:, 128 * b:128 * b + 128],
+                                             T.mc[:], T.mp[:], True, True))
+            out.append((k, m))
+        return out
+
+    def picks(i, Z, li):
+        pw, gg = T["pw%d" % i], T["gg%d" % i]
+        win, out = [], []
+        for b, (k, m) in enumerate(Z):
+            q = "vs"[b % 2]
+            d, p = pw[:, TQ * b:TQ * b + TQ], T["ps%d" % k][:, TQ:2 * TQ]
+            after(q, m)
+            win.append(mark(q, g.vector.tensor_copy(d, p) if q == "v" else g.scalar.activation(d, p, COPY)))
+            if q == "s":
+                for c in (b - 1, b):
+                    after("s", win[c], li)
+                    out.append(mark("s", g.scalar.activation(gg[:, TQ * c:TQ * c + TQ],
+                                                             pw[:, TQ * c:TQ * c + TQ].indirect(T["of%d" % i][:, 16 * c:16 * c + 16]), COPY)))
+        return win, out
+
+    def adds(i, Z, G):
+        gg, ht = T["gg%d" % i], T["ht%d" % i]
+        for b, (k, m) in enumerate(Z):
+            after("v", m, G[1][b])
+            a = mark("v", g.vector.tensor_tensor(ht[:, b:4 * TQ:4], T["ps%d" % k][:, 0:TQ], gg[:, TQ * b:TQ * b + TQ], ADD))
+            drained[k] = (a, G[0][b])
+        return a
+
+    def finish(i, s, a):
+        ht = T["ht%d" % i]
+        after("v", a)
+        m = mark("v", g.vector.tensor_scalar(ht[:], ht[:], 0.0, 0.03125, MAX, MULT))
+        return quantise("a%d" % s, 0, TQ, ht[:], m)
+
+    def farewell():
+        after("g", ("v", done["v"]), ("s", done["s"]), ("t", done["t"]), ("sent", sent[0]))
+
+    if rank is None:
+        r = worker.index(core)
+        nxt, prv = local[r][1:]
+        s, s2 = mirror[r], mirror[nxt]
+        onward = [worker[prv], cores[nxt]]
+        after("g", ("p_in%d" % s, nOFF))
+        send([(ALL, "p_in%d" % s, T["kpi%d" % s][:], onward)])
+        li = lists(0, s, ("q_in", nON), ("p_in%d" % s, nOFF))
+        after("g", ("k_in%d" % s, 2 * nOFF))
+        for c in onward:
+            ship(ALL, "k_in%d" % s, "kv%d" % s, 0, 512, [c])
+        ship(ALL, "v_in%d" % s, "kv%d" % s, 512, KV, [cores[q] for q in local[r]])
+        for i, k, n in ((0, s, nOFF), (1, s2, nALL)):
+            if i:
+                li = lists(1, k, ("p_in%d" % k, nALL))
+            Z = products(k, ("m_in", 2 * nON), ("k_in%d" % k, 2 * n))
+            m = finish(i, k, adds(i, Z, picks(i, Z, li)))
+            after("g", m)
+            ship(ALL, "a_in%d" % k, "a%d" % k, 0, TQ, [cores[r]])
+        farewell()
+        return
+
+    r, nxt, prv = local[rank]
+    peers = [cores[nxt], cores[prv]]
+    away = worker[mirror[r]]
+    g.sync.dma_start(T["kpi%d" % r][:], T.kp[:]).then_inc(T.sem.l_p, 16)
+    g.sync.dma_start(T.kt[:], T.ky[:]).then_inc(T.sem.l_k, 16)
+    g.sync.dma_start(T.vt[:], T.vv[:]).then_inc(T.sem.l_v, 16)
+    for k in range(8):
+        g.scalar.dma_start(T.qpi[16 * k:16 * k + 16, :], T.qp[:]).then_inc(T.sem.l_q, 16)
+    g.scalar.dma_start(T.mt[:, 1024:2048], T.rt[:]).then_inc(T.sem.l_m, 16)
+    g.scalar.dma_start(T.mt[:, 0:1024], T.qx[:]).then_inc(T.sem.l_m, 16)
+    LP, LQ = ("l_p", 16), ("l_q", 16 * 8)
+    after("g", LP)
+    send([(OFF, "p_in%d" % r, T["kpi%d" % r][:], [away]), (ON, "p_in%d" % r, T["kpi%d" % r][:], peers)])
+    mk = quantise("kv%d" % r, 0, 512, T.kt[:], ("l_k", 16))
+    mv = quantise("kv%d" % r, 512, KV, T.vt[:], ("l_v", 16))
+    after("g", mk, mv)
+    ship(OFF, "k_in%d" % r, "kv%d" % r, 0, KV, [away])
+    after("v", ("l_m", 32))
+    mm = mark("v", g.vector.quantize_mx(T.mc[:], T.mp[:], T.mt[:]))
+    li = lists(0, r, LP, LQ)
+    after("g", LQ)
+    send([(ON, "q_in", T.qpi[:], [worker[r]])])
+    after("g", mm)
+    send([(ON, "m_in", T.mc[:].bitcast(dt.uint8), [worker[r]])])
+    send([(ON, "m_in", T.mp[:], [worker[r]])])
+    ship(ALL, "k_in%d" % r, "kv%d" % r, 0, KV, peers)
+
+    last = mirror[prv]
+    Z = products(r, mk, mm)
+    made = {r: finish(0, r, adds(0, Z, picks(0, Z, li)))}
+    li1 = lists(1, prv, ("p_in%d" % prv, nON))
+    li2 = lists(2, nxt, ("p_in%d" % nxt, nON))
+    Z = products(prv, ("k_in%d" % prv, 2 * nALL))
+    a1 = adds(1, Z, picks(1, Z, li1))
+    Z = products(nxt, ("k_in%d" % nxt, 2 * nALL))
+    G = picks(2, Z, li2)
+    made[prv] = finish(1, prv, a1)
+    a2 = adds(2, Z, G)
+    li3 = lists(3, last, ("p_in%d" % last, nALL))
+    Z = products(last, ("k_in%d" % last, 2 * nALL))
+    G = picks(3, Z, li3)
+    made[nxt] = finish(2, nxt, a2)
+    made[last] = finish(3, last, adds(3, Z, G))
+
+    order = [r, prv, nxt, mirror[r], last, mirror[nxt]]
+    for s in order:
+        if s == mirror[r] or s == mirror[nxt]:
+            after("t", ("v_in%d" % s, 2 * nALL), ("a_in%d" % s, 2 * nALL))
+        elif s == last:
+            after("t", ("v_in%d" % s, 2 * nALL), made[s])
+        else:
+            after("t", made[s])
+        m = mark("t", g.tensor.matmul_mx(T.ps7[:, 0:TQ], T["kvc%d" % s][:, 512:KV], T["kvp%d" % s][:, 512:KV],
+                                         T["ac%d" % s][:], T["ap%d" % s][:], s == order[0], s == order[-1]))
+    after("s", m)
+    m = mark("s", g.scalar.activation(T.ys[:], T.ps7[:, 0:TQ], COPY))
+    after("s", m)
+    g.scalar.dma_start(T.y[:], T.ys[:]).then_inc(T.sem.stored, 16)
+    after("g", ("stored", 16))
+    farewell()

@@ -5,7 +5,8 @@ NR, TQ, KV = 6, 256, 640
 F8 = "float8_e4m3fn_x4"
 SCRATCH = {
     "kt": ("sbuf", [128, 2048], "bfloat16"),
-    "mt": ("sbuf", [128, 2048], "bfloat16"),
+    "xt": ("sbuf", [128, 1024], "bfloat16"),
+    "rtt": ("sbuf", [128, 1024], "bfloat16"),
     "vt": ("sbuf", [128, 512], "bfloat16"),
     "mc": ("sbuf", [128, 512], F8), "mp": ("sbuf", [128, 512], "uint8"),
     "qpi": ("sbuf", [128, 16], "int32"),
@@ -27,8 +28,8 @@ for _i in range(NR):
 for _i in range(8):
     SCRATCH["ps%d" % _i] = ("psum", [128, 512], "float32")
 
-SEMAPHORES = (["l_p", "l_q", "l_k", "l_v", "l_m", "vs", "ss", "ts", "sent", "stored", "q_in", "m_in"]
-              + ["%s_in%d" % (n, i) for n in ("p", "k", "v", "a") for i in range(NR)])
+SEMAPHORES = (["l_p", "l_q", "l_k0", "l_k1", "l_v", "l_r", "l_x", "vs", "ss", "ts", "sent", "stored", "q_in", "m_in"]
+              + ["%s_in%d" % (n, i) for n in ("p", "kc", "kp", "v", "a") for i in range(NR)])
 
 
 def layout(T, topo):
@@ -82,25 +83,17 @@ def rank_program(g, core, T, topo):
             out.append(DstId(rid=rid, pnc=pid))
         return out
 
-    def send(trs):
+    def send(sem, src, *ways):
         g.remote_dma_fused([RemoteDMATransfer(dst_ids=ids(ds), dma_engine_mask=sum(1 << e for e in es), remote_sem=T.sem[sem],
-                                              srcs=[src], dsts=[src] * len(ds)) for es, sem, src, ds in trs], local_sem=T.sem.sent)
-        sent[0] += sum(len(es) for es, _, _, _ in trs)
+                                              srcs=[src], dsts=[src] * len(ds)) for es, ds in ways], local_sem=T.sem.sent)
+        sent[0] += sum(len(es) for es, _ in ways)
 
-    def cut(name, kind, a, b):
-        n = name[:-1] + kind + name[-1]
-        return T[n][:, a:b].bitcast(dt.uint8) if kind == "c" else T[n][:, a:b]
+    def codes(name, a, b):
+        return T[name][:, a:b].bitcast(dt.uint8)
 
-    def ship(es, sem, name, a, b, ds):
-        for kind in "cp":
-            send([(es, sem, cut(name, kind, a, b), ds)])
-
-    def quantise(name, a, b, src, *deps):
+    def quantise(c, p, a, b, src, *deps):
         after("v", *deps)
-        return mark("v", g.vector.quantize_mx(T[name[:-1] + "c" + name[-1]][:, a:b], T[name[:-1] + "p" + name[-1]][:, a:b], src))
-
-    banks = 7 if rank is not None else 8
-    drained, turn = [()] * 8, [0]
+        return mark("v", g.vector.quantize_mx(T[c][:, a:b], T[p][:, a:b], src))
 
     def lists(i, s, *deps):
         after("v", *deps)
@@ -112,45 +105,80 @@ def rank_program(g, core, T, topo):
         after("v", m)
         return mark("v", g.vector.tensor_scalar(T["of%d" % i][:], T["ot%d" % i][:], 255.0, None, MIN))
 
-    def products(s, *deps):
-        out = []
-        for b in range(4):
-            k = turn[0] % banks
-            turn[0] += 1
-            after("t", *drained[k], *deps)
-            m = mark("t", g.tensor.matmul_mx(T["ps%d" % k][:], T["kvc%d" % s][:, 128 * b:128 * b + 128], T["kvp%d" % s][:, 128 * b:128 * b + 128],
-                                             T.mc[:], T.mp[:], True, True))
-            out.append((k, m))
-        return out
+    banks = 7 if rank is not None else 8
+    drained, turn = [()] * 8, [0]
+    TI = {}
 
-    def picks(i, Z, li):
-        pw, gg = T["pw%d" % i], T["gg%d" % i]
-        win, out = [], []
-        for b, (k, m) in enumerate(Z):
-            q = "vs"[b % 2]
-            d, p = pw[:, TQ * b:TQ * b + TQ], T["ps%d" % k][:, TQ:2 * TQ]
-            after(q, m)
-            win.append(mark(q, g.vector.tensor_copy(d, p) if q == "v" else g.scalar.activation(d, p, COPY)))
-            if q == "s":
-                for c in (b - 1, b):
-                    after("s", win[c], li)
-                    out.append(mark("s", g.scalar.activation(gg[:, TQ * c:TQ * c + TQ],
-                                                             pw[:, TQ * c:TQ * c + TQ].indirect(T["of%d" % i][:, 16 * c:16 * c + 16]), COPY)))
-        return win, out
+    def product(s, b, a):
+        k = turn[0] % banks
+        turn[0] += 1
+        after("t", *drained[k])
+        return k, mark("t", g.tensor.matmul_mx(T["ps%d" % k][:, 0:TQ], T["kvc%d" % s][:, 128 * b:128 * b + 128], T["kvp%d" % s][:, 128 * b:128 * b + 128],
+                                               T.mc[:, a:a + TQ], T.mp[:, a:a + TQ], True, True))
 
-    def adds(i, Z, G):
-        gg, ht = T["gg%d" % i], T["ht%d" % i]
-        for b, (k, m) in enumerate(Z):
-            after("v", m, G[1][b])
-            a = mark("v", g.vector.tensor_tensor(ht[:, b:4 * TQ:4], T["ps%d" % k][:, 0:TQ], gg[:, TQ * b:TQ * b + TQ], ADD))
-            drained[k] = (a, G[0][b])
-        return a
+    def window(i, b, q):
+        t = TI[i]
+        k, m = t["P"][b]
+        d, p = T["pw%d" % i][:, TQ * b:TQ * b + TQ], T["ps%d" % k][:, 0:TQ]
+        after(q, m)
+        t["W"][b] = mark(q, g.vector.tensor_copy(d, p) if q == "v" else g.scalar.activation(d, p, COPY))
+        drained[k] = (t["W"][b],)
 
-    def finish(i, s, a):
-        ht = T["ht%d" % i]
+    def pick(i, b):
+        t = TI[i]
+        after("s", t["W"][b], t["li"])
+        t["G"][b] = mark("s", g.scalar.activation(T["gg%d" % i][:, TQ * b:TQ * b + TQ],
+                                                  T["pw%d" % i][:, TQ * b:TQ * b + TQ].indirect(T["of%d" % i][:, 16 * b:16 * b + 16]), COPY))
+
+    def begin(i, s, li, *deps):
+        after("t", *deps)
+        TI[i] = {"s": s, "li": li, "P": [product(s, b, TQ) for b in range(4)], "S": {}, "W": {}, "G": {}}
+
+    def scores(i, *deps):
+        after("t", *deps)
+        TI[i]["S"] = [product(TI[i]["s"], b, 0) for b in range(4)]
+
+    def add(i, b):
+        t, ht = TI[i], T["ht%d" % i]
+        k, m = t["S"][b]
+        after("v", m, t["G"][b])
+        h = ht[:, b:4 * TQ:4]
+        a = mark("v", g.vector.tensor_tensor(h, T["ps%d" % k][:, 0:TQ], T["gg%d" % i][:, TQ * b:TQ * b + TQ], ADD))
+        drained[k] = (a,)
         after("v", a)
-        m = mark("v", g.vector.tensor_scalar(ht[:], ht[:], 0.0, 0.03125, MAX, MULT))
-        return quantise("a%d" % s, 0, TQ, ht[:], m)
+        t["R"] = mark("v", g.vector.tensor_scalar(h, h, 0.0, 0.03125, MAX, MULT))
+
+    def pack(i):
+        s = TI[i]["s"]
+        return quantise("ac%d" % s, "ap%d" % s, 0, TQ, T["ht%d" % i][:], TI[i]["R"])
+
+    def alone(i, *deps):
+        for b in range(4):
+            window(i, b, "v")
+            pick(i, b)
+        scores(i, *deps)
+
+    def follow(i, start):
+        for b in range(3):
+            add(i, b)
+        start()
+        window(i + 1, 0, "v")
+        window(i + 1, 1, "s")
+        pick(i + 1, 0)
+        pick(i + 1, 1)
+        add(i, 3)
+        window(i + 1, 2, "v")
+        window(i + 1, 3, "s")
+        pick(i + 1, 2)
+        pick(i + 1, 3)
+        m = pack(i)
+        scores(i + 1)
+        return m
+
+    def close(i):
+        for b in range(4):
+            add(i, b)
+        return pack(i)
 
     def farewell():
         after("g", ("v", done["v"]), ("s", done["s"]), ("t", done["t"]), ("sent", sent[0]))
@@ -159,76 +187,84 @@ def rank_program(g, core, T, topo):
         r = worker.index(core)
         nxt, prv = local[r][1:]
         s, s2 = mirror[r], mirror[nxt]
-        onward = [worker[prv], cores[nxt]]
+        w, n = (ALL, [worker[prv]]), (ALL, [cores[nxt]])
+        home, mine = (ALL, [cores[q] for q in local[r]]), (ALL, [cores[r]])
         after("g", ("p_in%d" % s, nOFF))
-        send([(ALL, "p_in%d" % s, T["kpi%d" % s][:], onward)])
-        li = lists(0, s, ("q_in", nON), ("p_in%d" % s, nOFF))
-        after("g", ("k_in%d" % s, 2 * nOFF))
-        for c in onward:
-            ship(ALL, "k_in%d" % s, "kv%d" % s, 0, 512, [c])
-        ship(ALL, "v_in%d" % s, "kv%d" % s, 512, KV, [cores[q] for q in local[r]])
-        for i, k, n in ((0, s, nOFF), (1, s2, nALL)):
-            if i:
-                li = lists(1, k, ("p_in%d" % k, nALL))
-            Z = products(k, ("m_in", 2 * nON), ("k_in%d" % k, 2 * n))
-            m = finish(i, k, adds(i, Z, picks(i, Z, li)))
+        send("p_in%d" % s, T["kpi%d" % s][:], (ALL, [worker[prv], cores[nxt]]))
+        li = lists(0, s, ("q_in", nOFF), ("p_in%d" % s, nOFF))
+        after("g", ("kc_in%d" % s, nOFF))
+        send("kc_in%d" % s, codes("kvc%d" % s, 0, 512), w)
+        after("g", ("kp_in%d" % s, nOFF))
+        send("kp_in%d" % s, T["kvp%d" % s][:, 0:512], w)
+        send("kc_in%d" % s, codes("kvc%d" % s, 0, 512), n)
+        send("kp_in%d" % s, T["kvp%d" % s][:, 0:512], n)
+        after("g", ("v_in%d" % s, 2 * nOFF))
+        send("v_in%d" % s, codes("kvc%d" % s, 512, KV), home)
+        send("v_in%d" % s, T["kvp%d" % s][:, 512:KV], home)
+
+        def deliver(k, m):
             after("g", m)
-            ship(ALL, "a_in%d" % k, "a%d" % k, 0, TQ, [cores[r]])
+            send("a_in%d" % k, codes("ac%d" % k, 0, TQ), mine)
+            send("a_in%d" % k, T["ap%d" % k][:, 0:TQ], mine)
+
+        begin(0, s, li, ("m_in", 2 * nALL), ("kc_in%d" % s, nOFF), ("kp_in%d" % s, nOFF))
+        alone(0)
+        deliver(s, follow(0, lambda: begin(1, s2, lists(1, s2, ("p_in%d" % s2, nALL)), ("kc_in%d" % s2, nALL), ("kp_in%d" % s2, nALL))))
+        deliver(s2, close(1))
         farewell()
         return
 
     r, nxt, prv = local[rank]
-    peers = [cores[nxt], cores[prv]]
-    away = worker[mirror[r]]
+    away, mine = (OFF, [worker[mirror[r]]]), [worker[r]]
+    kvc, kvp = "kvc%d" % r, "kvp%d" % r
     g.sync.dma_start(T["kpi%d" % r][:], T.kp[:]).then_inc(T.sem.l_p, 16)
-    g.sync.dma_start(T.kt[:], T.ky[:]).then_inc(T.sem.l_k, 16)
-    g.sync.dma_start(T.vt[:], T.vv[:]).then_inc(T.sem.l_v, 16)
+    for i in range(2):
+        g.sync.dma_start(T.kt[:, 1024 * i:1024 * i + 1024], T.ky[:, 1024 * i:1024 * i + 1024]).then_inc(T.sem["l_k%d" % i], 16)
     for k in range(8):
         g.scalar.dma_start(T.qpi[16 * k:16 * k + 16, :], T.qp[:]).then_inc(T.sem.l_q, 16)
-    g.scalar.dma_start(T.mt[:, 1024:2048], T.rt[:]).then_inc(T.sem.l_m, 16)
-    g.scalar.dma_start(T.mt[:, 0:1024], T.qx[:]).then_inc(T.sem.l_m, 16)
+    g.scalar.dma_start(T.rtt[:], T.rt[:]).then_inc(T.sem.l_r, 16)
+    g.scalar.dma_start(T.xt[:], T.qx[:]).then_inc(T.sem.l_x, 16)
+    g.scalar.dma_start(T.vt[:], T.vv[:]).then_inc(T.sem.l_v, 16)
     LP, LQ = ("l_p", 16), ("l_q", 16 * 8)
     after("g", LP)
-    send([(OFF, "p_in%d" % r, T["kpi%d" % r][:], [away]), (ON, "p_in%d" % r, T["kpi%d" % r][:], peers)])
-    mk = quantise("kv%d" % r, 0, 512, T.kt[:], ("l_k", 16))
-    mv = quantise("kv%d" % r, 512, KV, T.vt[:], ("l_v", 16))
-    after("g", mk, mv)
-    ship(OFF, "k_in%d" % r, "kv%d" % r, 0, KV, [away])
-    after("v", ("l_m", 32))
-    mm = mark("v", g.vector.quantize_mx(T.mc[:], T.mp[:], T.mt[:]))
+    send("p_in%d" % r, T["kpi%d" % r][:], away, (ON, [cores[nxt], cores[prv]]))
+    for i in range(2):
+        mk = quantise(kvc, kvp, 256 * i, 256 * i + 256, T.kt[:, 1024 * i:1024 * i + 1024], ("l_k%d" % i, 16))
+    after("g", mk)
+    send("kc_in%d" % r, codes(kvc, 0, 512), away, (ON, [cores[nxt]]))
+    send("kp_in%d" % r, T[kvp][:, 0:512], away, (ON, [cores[nxt]]))
     li = lists(0, r, LP, LQ)
+    mr = quantise("mc", "mp", TQ, 2 * TQ, T.rtt[:], ("l_r", 16))
+    mx = quantise("mc", "mp", 0, TQ, T.xt[:], ("l_x", 16))
     after("g", LQ)
-    send([(ON, "q_in", T.qpi[:], [worker[r]])])
-    after("g", mm)
-    send([(ON, "m_in", T.mc[:].bitcast(dt.uint8), [worker[r]])])
-    send([(ON, "m_in", T.mp[:], [worker[r]])])
-    ship(ALL, "k_in%d" % r, "kv%d" % r, 0, KV, peers)
+    send("q_in", T.qpi[:], (OFF, mine))
+    after("g", mr, mx)
+    send("m_in", codes("mc", 0, 512), (ALL, mine))
+    send("m_in", T.mp[:], (ALL, mine))
+    send("kc_in%d" % r, codes(kvc, 0, 512), (ALL, [cores[prv]]))
+    send("kp_in%d" % r, T[kvp][:, 0:512], (ALL, [cores[prv]]))
 
     last = mirror[prv]
-    Z = products(r, mk, mm)
-    made = {r: finish(0, r, adds(0, Z, picks(0, Z, li)))}
+    begin(0, r, li, mk, mr)
+    alone(0, mx)
+    mv = quantise(kvc, kvp, 512, KV, T.vt[:], ("l_v", 16))
+    after("g", mv)
+    send("v_in%d" % r, codes(kvc, 512, KV), away, (ON, [cores[nxt], cores[prv]]))
+    send("v_in%d" % r, T[kvp][:, 512:KV], away, (ON, [cores[nxt], cores[prv]]))
+    made = {r: close(0)}
     li1 = lists(1, prv, ("p_in%d" % prv, nON))
     li2 = lists(2, nxt, ("p_in%d" % nxt, nON))
-    Z = products(prv, ("k_in%d" % prv, 2 * nALL))
-    a1 = adds(1, Z, picks(1, Z, li1))
-    Z = products(nxt, ("k_in%d" % nxt, 2 * nALL))
-    G = picks(2, Z, li2)
-    made[prv] = finish(1, prv, a1)
-    a2 = adds(2, Z, G)
-    li3 = lists(3, last, ("p_in%d" % last, nALL))
-    Z = products(last, ("k_in%d" % last, 2 * nALL))
-    G = picks(3, Z, li3)
-    made[nxt] = finish(2, nxt, a2)
-    made[last] = finish(3, last, adds(3, Z, G))
+    begin(1, prv, li1, ("kc_in%d" % prv, nON), ("kp_in%d" % prv, nON))
+    alone(1)
+    made[prv] = follow(1, lambda: begin(2, nxt, li2, ("kc_in%d" % nxt, nALL), ("kp_in%d" % nxt, nALL)))
+    made[nxt] = follow(2, lambda: begin(3, last, lists(3, last, ("p_in%d" % last, nALL)), ("kc_in%d" % last, nALL), ("kp_in%d" % last, nALL)))
+    made[last] = close(3)
 
     order = [r, prv, nxt, mirror[r], last, mirror[nxt]]
     for s in order:
-        if s == mirror[r] or s == mirror[nxt]:
-            after("t", ("v_in%d" % s, 2 * nALL), ("a_in%d" % s, 2 * nALL))
-        elif s == last:
-            after("t", ("v_in%d" % s, 2 * nALL), made[s])
-        else:
-            after("t", made[s])
+        if s != r:
+            after("t", ("v_in%d" % s, 2 * (nON if s in (prv, nxt) else nALL)))
+        after("t", made[s] if s in made else ("a_in%d" % s, 2 * nALL))
         m = mark("t", g.tensor.matmul_mx(T.ps7[:, 0:TQ], T["kvc%d" % s][:, 512:KV], T["kvp%d" % s][:, 512:KV],
                                          T["ac%d" % s][:], T["ap%d" % s][:], s == order[0], s == order[-1]))
     after("s", m)

@@ -1,35 +1,43 @@
 from concourse.bass import DstId, RemoteDMATransfer
 from concourse.mybir import dt, AluOpType, ActivationFunctionType
 
-NR, TQ, KV = 6, 256, 640
+NR, TQ = 6, 256
 F8 = "float8_e4m3fn_x4"
+RT, OWN, PRV, NXT = 0, 256, 512, 768
 SCRATCH = {
     "kt": ("sbuf", [128, 2048], "bfloat16"),
     "xt": ("sbuf", [128, 1024], "bfloat16"),
     "rtt": ("sbuf", [128, 1024], "bfloat16"),
     "vt": ("sbuf", [128, 512], "bfloat16"),
-    "mc": ("sbuf", [128, 512], F8), "mp": ("sbuf", [128, 512], "uint8"),
-    "qpi": ("sbuf", [128, 16], "int32"),
+    "mc": ("sbuf", [128, 1024], F8), "mp": ("sbuf", [128, 1024], "uint8"),
+    "kco": ("sbuf", [128, 512], F8), "kpo": ("sbuf", [128, 512], "uint8"),
+    "kcf": ("sbuf", [128, 512], F8), "kpf": ("sbuf", [128, 512], "uint8"),
+    "kpi": ("sbuf", [128, 4], "int32"),
+    "kfo": ("sbuf", [128, 4], "float32"), "kff": ("sbuf", [128, 4], "float32"),
+    "qpi": ("sbuf", [128, 48], "int32"),
+    "pwo": ("sbuf", [128, 1024], "float32"), "pwf": ("sbuf", [128, 1024], "float32"),
     "ys": ("sbuf", [128, 256], "float32"),
 }
+for _n, _w in (("o", 64), ("x", 128), ("f", 64)):
+    SCRATCH["ot" + _n] = ("sbuf", [128, _w], "float32")
+    SCRATCH["of" + _n] = ("sbuf", [128, _w], "uint16")
 for _i in range(4):
-    SCRATCH["pw%d" % _i] = ("sbuf", [128, 1024], "float32")
     SCRATCH["gg%d" % _i] = ("sbuf", [128, 1024], "float32")
     SCRATCH["ht%d" % _i] = ("sbuf", [128, 1024], "bfloat16")
-    SCRATCH["kf%d" % _i] = ("sbuf", [128, 4], "float32")
-    SCRATCH["ot%d" % _i] = ("sbuf", [128, 64], "float32")
-    SCRATCH["of%d" % _i] = ("sbuf", [128, 64], "uint16")
+for _i in range(2):
+    SCRATCH["oc%d" % _i] = ("sbuf", [128, TQ], F8)
+    SCRATCH["op%d" % _i] = ("sbuf", [128, TQ], "uint8")
 for _i in range(NR):
-    SCRATCH["kvc%d" % _i] = ("sbuf", [128, KV], F8)
-    SCRATCH["kvp%d" % _i] = ("sbuf", [128, KV], "uint8")
+    SCRATCH["vc%d" % _i] = ("sbuf", [128, 128], F8)
+    SCRATCH["vp%d" % _i] = ("sbuf", [128, 128], "uint8")
     SCRATCH["ac%d" % _i] = ("sbuf", [128, TQ], F8)
     SCRATCH["ap%d" % _i] = ("sbuf", [128, TQ], "uint8")
-    SCRATCH["kpi%d" % _i] = ("sbuf", [128, 4], "int32")
 for _i in range(8):
     SCRATCH["ps%d" % _i] = ("psum", [128, 512], "float32")
 
-SEMAPHORES = (["l_p", "l_q", "l_k0", "l_k1", "l_v", "l_r", "l_x", "vs", "ss", "ts", "sent", "stored", "q_in", "m_in"]
-              + ["%s_in%d" % (n, i) for n in ("p", "kc", "kp", "v", "a") for i in range(NR)])
+SEMAPHORES = (["l_p", "l_q", "l_k0", "l_k1", "l_v", "l_r", "l_x", "vs", "ss", "ts", "sent", "stored",
+               "q_in", "kf_in", "k0_in", "k1_in", "r_in", "xp_in", "xn_in"]
+              + ["%s_in%d" % (n, i) for n in ("v", "a") for i in range(NR)])
 
 
 def layout(T, topo):
@@ -52,6 +60,8 @@ def rank_program(g, core, T, topo):
     rank = T.rank_of(core)
     if rank is None and core not in worker:
         return
+    r, nxt, prv = local[rank if rank is not None else worker.index(core)]
+    far_s = mirror[r]
     ADD, MAX, MIN, MULT, SUB = AluOpType.add, AluOpType.max, AluOpType.min, AluOpType.mult, AluOpType.subtract
     COPY = ActivationFunctionType.Copy
     eng = {"g": g, "v": g.vector, "s": g.scalar, "t": g.tensor}
@@ -83,190 +93,220 @@ def rank_program(g, core, T, topo):
             out.append(DstId(rid=rid, pnc=pid))
         return out
 
-    def send(sem, src, *ways):
+    def send(sems, src, *ways):
+        if not isinstance(sems, list):
+            sems = [sems] * len(ways)
         g.remote_dma_fused([RemoteDMATransfer(dst_ids=ids(ds), dma_engine_mask=sum(1 << e for e in es), remote_sem=T.sem[sem],
-                                              srcs=[src], dsts=[src] * len(ds)) for es, ds in ways], local_sem=T.sem.sent)
-        sent[0] += sum(len(es) for es, _ in ways)
+                                              srcs=[src], dsts=[to] * len(ds)) for sem, (es, ds, to) in zip(sems, ways)], local_sem=T.sem.sent)
+        sent[0] += sum(len(es) for es, _, _ in ways)
 
     def codes(name, a, b):
         return T[name][:, a:b].bitcast(dt.uint8)
 
-    def quantise(c, p, a, b, src, *deps):
-        after("v", *deps)
-        return mark("v", g.vector.quantize_mx(T[c][:, a:b], T[p][:, a:b], src))
+    def plane(name, a, b):
+        return T[name][:, a:b]
 
-    def lists(i, s, *deps):
+    def ship(sems, src, a, n, *ways):
+        for k, view in ((0, codes), (1, plane)):
+            send(sems, view(src[k], a, a + n), *[(es, ds, view(to[k], ta, ta + n)) for es, ds, to, ta in ways])
+
+    M, KO, KF = ("mc", "mp"), ("kco", "kpo"), ("kcf", "kpf")
+
+    def V(s):
+        return ("vc%d" % s, "vp%d" % s)
+
+    def A(s):
+        return ("ac%d" % s, "ap%d" % s)
+
+    def quantise(to, a, b, src, *deps):
         after("v", *deps)
-        kf = T["kf%d" % i]
-        m = mark("v", g.vector.tensor_scalar(kf[:], T["kpi%d" % s][:], 128.0, None, SUB))
-        after("v", m)
+        return mark("v", g.vector.quantize_mx(T[to[0]][:, a:b], T[to[1]][:, a:b], src))
+
+    def lists(n, kf, a, w, *deps):
+        after("v", *deps)
         for b in range(4):
-            m = mark("v", g.vector.tensor_scalar(T["ot%d" % i][:, 16 * b:16 * b + 16], T.qpi[:], kf[:, b:b + 1], 0.0, SUB, MAX))
+            m = mark("v", g.vector.tensor_scalar(T["ot" + n][:, w * b:w * b + w], T.qpi[:, a:a + w], T[kf][:, b:b + 1], 0.0, SUB, MAX))
         after("v", m)
-        return mark("v", g.vector.tensor_scalar(T["of%d" % i][:], T["ot%d" % i][:], 255.0, None, MIN))
+        return mark("v", g.vector.tensor_scalar(T["of" + n][:], T["ot" + n][:], 255.0, None, MIN))
 
     banks = 7 if rank is not None else 8
     drained, turn = [()] * 8, [0]
-    TI = {}
+    P, W, S, G, R = {}, {}, {}, {}, {}
 
-    def product(s, b, a):
+    def product(K, b, a):
         k = turn[0] % banks
         turn[0] += 1
         after("t", *drained[k])
-        return k, mark("t", g.tensor.matmul_mx(T["ps%d" % k][:, 0:TQ], T["kvc%d" % s][:, 128 * b:128 * b + 128], T["kvp%d" % s][:, 128 * b:128 * b + 128],
+        return k, mark("t", g.tensor.matmul_mx(T["ps%d" % k][:, 0:TQ], T[K[0]][:, 128 * b:128 * b + 128], T[K[1]][:, 128 * b:128 * b + 128],
                                                T.mc[:, a:a + TQ], T.mp[:, a:a + TQ], True, True))
 
-    def window(i, b, q):
-        t = TI[i]
-        k, m = t["P"][b]
-        d, p = T["pw%d" % i][:, TQ * b:TQ * b + TQ], T["ps%d" % k][:, 0:TQ]
+    def distances(n, K, bs, *deps):
+        after("t", *deps)
+        for b in bs:
+            P[n, b] = product(K, b, RT)
+
+    def scores(i, K, a, *deps):
+        after("t", *deps)
+        for b in range(4):
+            S[i, b] = product(K, b, a)
+
+    def window(n, b, q):
+        k, m = P[n, b]
+        d, p = T["pw" + n][:, TQ * b:TQ * b + TQ], T["ps%d" % k][:, 0:TQ]
         after(q, m)
-        t["W"][b] = mark(q, g.vector.tensor_copy(d, p) if q == "v" else g.scalar.activation(d, p, COPY))
-        drained[k] = (t["W"][b],)
+        W[n, b] = mark(q, g.vector.tensor_copy(d, p) if q == "v" else g.scalar.activation(d, p, COPY))
+        drained[k] = (W[n, b],)
 
-    def pick(i, b):
-        t = TI[i]
-        after("s", t["W"][b], t["li"])
-        t["G"][b] = mark("s", g.scalar.activation(T["gg%d" % i][:, TQ * b:TQ * b + TQ],
-                                                  T["pw%d" % i][:, TQ * b:TQ * b + TQ].indirect(T["of%d" % i][:, 16 * b:16 * b + 16]), COPY))
-
-    def begin(i, s, li, *deps):
-        after("t", *deps)
-        TI[i] = {"s": s, "li": li, "P": [product(s, b, TQ) for b in range(4)], "S": {}, "W": {}, "G": {}}
-
-    def scores(i, *deps):
-        after("t", *deps)
-        TI[i]["S"] = [product(TI[i]["s"], b, 0) for b in range(4)]
+    def pick(i, n, b, of, col, li):
+        after("s", W[n, b], li)
+        G[i, b] = mark("s", g.scalar.activation(T["gg%d" % i][:, TQ * b:TQ * b + TQ],
+                                                T["pw" + n][:, TQ * b:TQ * b + TQ].indirect(T[of][:, col:col + 16]), COPY))
 
     def add(i, b):
-        t, ht = TI[i], T["ht%d" % i]
-        k, m = t["S"][b]
-        after("v", m, t["G"][b])
-        h = ht[:, b:4 * TQ:4]
-        a = mark("v", g.vector.tensor_tensor(h, T["ps%d" % k][:, 0:TQ], T["gg%d" % i][:, TQ * b:TQ * b + TQ], ADD))
-        drained[k] = (a,)
-        after("v", a)
-        t["R"] = mark("v", g.vector.tensor_scalar(h, h, 0.0, 0.03125, MAX, MULT))
+        k, m = S[i, b]
+        after("v", m, G[i, b])
+        R[i, b] = mark("v", g.vector.tensor_tensor(T["ht%d" % i][:, b:4 * TQ:4], T["ps%d" % k][:, 0:TQ], T["gg%d" % i][:, TQ * b:TQ * b + TQ], ADD))
+        drained[k] = (R[i, b],)
 
-    def pack(i):
-        s = TI[i]["s"]
-        return quantise("ac%d" % s, "ap%d" % s, 0, TQ, T["ht%d" % i][:], TI[i]["R"])
+    def relu(i, b, step):
+        after("v", *[R[i, c] for c in range(b, 4, step)])
+        h = T["ht%d" % i][:, b:4 * TQ:step]
+        R[i] = mark("v", g.vector.tensor_scalar(h, h, 0.0, 0.03125, MAX, MULT))
 
-    def alone(i, *deps):
-        for b in range(4):
-            window(i, b, "v")
-            pick(i, b)
-        scores(i, *deps)
+    def pack(i, to):
+        return quantise(to, 0, TQ, T["ht%d" % i][:], R[i])
 
-    def follow(i, start):
-        for b in range(3):
-            add(i, b)
-        start()
-        window(i + 1, 0, "v")
-        window(i + 1, 1, "s")
-        pick(i + 1, 0)
-        pick(i + 1, 1)
-        add(i, 3)
-        window(i + 1, 2, "v")
-        window(i + 1, 3, "s")
-        pick(i + 1, 2)
-        pick(i + 1, 3)
-        m = pack(i)
-        scores(i + 1)
+    def lace(i, j, to):
+        add(j, 0)
+        relu(i, 0, 1)
+        add(j, 1)
+        m = pack(i, to)
+        add(j, 2)
         return m
 
-    def close(i):
-        for b in range(4):
-            add(i, b)
-        return pack(i)
+    def close(i, to):
+        relu(i, 0, 2)
+        add(i, 3)
+        relu(i, 1, 2)
+        return pack(i, to)
 
     def farewell():
         after("g", ("v", done["v"]), ("s", done["s"]), ("t", done["t"]), ("sent", sent[0]))
 
+    B = range(4)
+    QIN = ("q_in", nON + nOFF)
     if rank is None:
-        r = worker.index(core)
-        nxt, prv = local[r][1:]
-        s, s2 = mirror[r], mirror[nxt]
-        w, n = (ALL, [worker[prv]]), (ALL, [cores[nxt]])
-        home, mine = (ALL, [cores[q] for q in local[r]]), (ALL, [cores[r]])
-        after("g", ("p_in%d" % s, nOFF))
-        send("p_in%d" % s, T["kpi%d" % s][:], (ALL, [worker[prv], cores[nxt]]))
-        li = lists(0, s, ("q_in", nOFF), ("p_in%d" % s, nOFF))
-        after("g", ("kc_in%d" % s, nOFF))
-        send("kc_in%d" % s, codes("kvc%d" % s, 0, 512), w)
-        after("g", ("kp_in%d" % s, nOFF))
-        send("kp_in%d" % s, T["kvp%d" % s][:, 0:512], w)
-        send("kc_in%d" % s, codes("kvc%d" % s, 0, 512), n)
-        send("kp_in%d" % s, T["kvp%d" % s][:, 0:512], n)
-        after("g", ("v_in%d" % s, 2 * nOFF))
-        send("v_in%d" % s, codes("kvc%d" % s, 512, KV), home)
-        send("v_in%d" % s, T["kvp%d" % s][:, 512:KV], home)
+        here, home = [cores[r]], [cores[q] for q in local[r]]
+        KFIN = ("kf_in", nOFF)
+        after("g", KFIN)
+        send("kf_in", T.kff[:], (ALL, here, T.kff[:]))
+        for i in range(2):
+            after("g", ("k%d_in" % i, 2 * nOFF))
+            ship("k%d_in" % i, KF, 256 * i, 256, (ALL, here, KF, 256 * i))
+        after("g", ("v_in%d" % far_s, 2 * nOFF))
+        ship("v_in%d" % far_s, V(far_s), 0, 128, (ALL, home, V(far_s), 0))
 
-        def deliver(k, m):
-            after("g", m)
-            send("a_in%d" % k, codes("ac%d" % k, 0, TQ), mine)
-            send("a_in%d" % k, T["ap%d" % k][:, 0:TQ], mine)
-
-        begin(0, s, li, ("m_in", 2 * nALL), ("kc_in%d" % s, nOFF), ("kp_in%d" % s, nOFF))
-        alone(0)
-        deliver(s, follow(0, lambda: begin(1, s2, lists(1, s2, ("p_in%d" % s2, nALL)), ("kc_in%d" % s2, nALL), ("kp_in%d" % s2, nALL))))
-        deliver(s2, close(1))
+        li = lists("x", "kff", 16, 32, QIN, KFIN)
+        distances("f", KF, (0, 1), ("r_in", 2 * nON), ("k0_in", 2 * nOFF))
+        distances("f", KF, (2, 3), ("k1_in", 2 * nOFF))
+        window("f", 0, "s")
+        for b in (1, 2, 3):
+            window("f", b, "v")
+        for i in range(2):
+            for b in B:
+                pick(i, "f", b, "ofx", 32 * b + 16 * i, li)
+        scores(0, KF, PRV, ("xp_in", 2 * nON))
+        for b in B:
+            add(0, b)
+        scores(1, KF, NXT, ("xn_in", 2 * nOFF))
+        made = [lace(0, 1, ("oc0", "op0")), close(1, ("oc1", "op1"))]
+        for i, q in ((0, prv), (1, nxt)):
+            after("g", made[i])
+            ship("a_in%d" % far_s, ("oc%d" % i, "op%d" % i), 0, TQ, (ALL, [cores[q]], A(far_s), 0))
         farewell()
         return
 
-    r, nxt, prv = local[rank]
-    away, mine = (OFF, [worker[mirror[r]]]), [worker[r]]
-    kvc, kvp = "kvc%d" % r, "kvp%d" % r
-    g.sync.dma_start(T["kpi%d" % r][:], T.kp[:]).then_inc(T.sem.l_p, 16)
+    away, mine = [worker[far_s]], [worker[r]]
+    to_nxt, to_prv = [cores[nxt], worker[nxt]], [cores[prv], worker[prv]]
+    g.sync.dma_start(T.kpi[:], T.kp[:]).then_inc(T.sem.l_p, 16)
     for i in range(2):
         g.sync.dma_start(T.kt[:, 1024 * i:1024 * i + 1024], T.ky[:, 1024 * i:1024 * i + 1024]).then_inc(T.sem["l_k%d" % i], 16)
+    g.sync.dma_start(T.rtt[:], T.rt[:]).then_inc(T.sem.l_r, 16)
     for k in range(8):
-        g.scalar.dma_start(T.qpi[16 * k:16 * k + 16, :], T.qp[:]).then_inc(T.sem.l_q, 16)
-    g.scalar.dma_start(T.rtt[:], T.rt[:]).then_inc(T.sem.l_r, 16)
+        g.scalar.dma_start(T.qpi[16 * k:16 * k + 16, 0:16], T.qp[:]).then_inc(T.sem.l_q, 16)
     g.scalar.dma_start(T.xt[:], T.qx[:]).then_inc(T.sem.l_x, 16)
     g.scalar.dma_start(T.vt[:], T.vv[:]).then_inc(T.sem.l_v, 16)
-    LP, LQ = ("l_p", 16), ("l_q", 16 * 8)
-    after("g", LP)
-    send("p_in%d" % r, T["kpi%d" % r][:], away, (ON, [cores[nxt], cores[prv]]))
-    for i in range(2):
-        mk = quantise(kvc, kvp, 256 * i, 256 * i + 256, T.kt[:, 1024 * i:1024 * i + 1024], ("l_k%d" % i, 16))
-    after("g", mk)
-    send("kc_in%d" % r, codes(kvc, 0, 512), away, (ON, [cores[nxt]]))
-    send("kp_in%d" % r, T[kvp][:, 0:512], away, (ON, [cores[nxt]]))
-    li = lists(0, r, LP, LQ)
-    mr = quantise("mc", "mp", TQ, 2 * TQ, T.rtt[:], ("l_r", 16))
-    mx = quantise("mc", "mp", 0, TQ, T.xt[:], ("l_x", 16))
+    LQ = ("l_q", 16 * 8)
+
+    after("v", ("l_p", 16))
+    mf = mark("v", g.vector.tensor_scalar(T.kfo[:], T.kpi[:], 128.0, None, SUB))
+    after("g", mf)
+    send("kf_in", T.kfo[:], (OFF, away, T.kff[:]))
     after("g", LQ)
-    send("q_in", T.qpi[:], (OFF, mine))
-    after("g", mr, mx)
-    send("m_in", codes("mc", 0, 512), (ALL, mine))
-    send("m_in", T.mp[:], (ALL, mine))
-    send("kc_in%d" % r, codes(kvc, 0, 512), (ALL, [cores[prv]]))
-    send("kp_in%d" % r, T[kvp][:, 0:512], (ALL, [cores[prv]]))
+    send("q_in", T.qpi[:, 0:16], (ON, to_nxt, T.qpi[:, 16:32]), (OFF, to_prv, T.qpi[:, 32:48]))
+    for i in range(2):
+        mk = quantise(KO, 256 * i, 256 * i + 256, T.kt[:, 1024 * i:1024 * i + 1024], ("l_k%d" % i, 16))
+        after("g", mk)
+        ship("k%d_in" % i, KO, 256 * i, 256, (OFF, away, KF, 256 * i))
+    lo = lists("o", "kfo", 0, 16, mf, LQ)
+    mr = quantise(M, RT, RT + TQ, T.rtt[:], ("l_r", 16))
+    after("g", mr)
+    ship("r_in", M, RT, TQ, (ON, mine, M, RT))
+    mx = quantise(M, OWN, OWN + TQ, T.xt[:], ("l_x", 16))
+    after("g", mx)
+    ship(["xp_in", "xn_in"], M, OWN, TQ, (ON, to_nxt, M, PRV), (OFF, to_prv, M, NXT))
 
-    last = mirror[prv]
-    begin(0, r, li, mk, mr)
-    alone(0, mx)
-    mv = quantise(kvc, kvp, 512, KV, T.vt[:], ("l_v", 16))
+    distances("o", KO, B, mk, mr)
+    for b, q in ((0, "s"), (1, "s"), (2, "v"), (3, "v")):
+        window("o", b, q)
+    scores(0, KO, OWN, mx)
+    for b in B:
+        pick(0, "o", b, "ofo", 16 * b, lo)
+    add(0, 0)
+    lx = lists("x", "kfo", 16, 32, QIN)
+    for i in range(2):
+        for b in B:
+            pick(1 + i, "o", b, "ofx", 32 * b + 16 * i, lx)
+    add(0, 1)
+    mv = quantise(V(r), 0, 128, T.vt[:], ("l_v", 16))
     after("g", mv)
-    send("v_in%d" % r, codes(kvc, 512, KV), away, (ON, [cores[nxt], cores[prv]]))
-    send("v_in%d" % r, T[kvp][:, 512:KV], away, (ON, [cores[nxt], cores[prv]]))
-    made = {r: close(0)}
-    li1 = lists(1, prv, ("p_in%d" % prv, nON))
-    li2 = lists(2, nxt, ("p_in%d" % nxt, nON))
-    begin(1, prv, li1, ("kc_in%d" % prv, nON), ("kp_in%d" % prv, nON))
-    alone(1)
-    made[prv] = follow(1, lambda: begin(2, nxt, li2, ("kc_in%d" % nxt, nALL), ("kp_in%d" % nxt, nALL)))
-    made[nxt] = follow(2, lambda: begin(3, last, lists(3, last, ("p_in%d" % last, nALL)), ("kc_in%d" % last, nALL), ("kp_in%d" % last, nALL)))
-    made[last] = close(3)
+    ship("v_in%d" % r, V(r), 0, 128, (OFF, away, V(r), 0), (ON, [cores[nxt], cores[prv]], V(r), 0))
+    add(0, 2)
+    add(0, 3)
+    scores(1, KO, PRV, ("xp_in", 2 * nON))
+    made = {r: lace(0, 1, A(r))}
+    lf = lists("f", "kff", 0, 16, ("kf_in", nALL))
+    add(1, 3)
+    scores(2, KO, NXT, ("xn_in", 2 * nOFF))
+    m1 = lace(1, 2, ("oc0", "op0"))
+    add(2, 3)
+    relu(2, 0, 1)
+    m2 = pack(2, ("oc1", "op1"))
+    for i, q, m in ((0, prv, m1), (1, nxt, m2)):
+        after("g", m)
+        ship("a_in%d" % r, ("oc%d" % i, "op%d" % i), 0, TQ, (ALL, [cores[q]], A(r), 0))
 
-    order = [r, prv, nxt, mirror[r], last, mirror[nxt]]
-    for s in order:
-        if s != r:
-            after("t", ("v_in%d" % s, 2 * (nON if s in (prv, nxt) else nALL)))
+    order = [r, nxt, prv, mirror[nxt], far_s, mirror[prv]]
+
+    def value(s):
+        after("t", mv if s == r else ("v_in%d" % s, 2 * (nON if s in (prv, nxt) else nALL)))
         after("t", made[s] if s in made else ("a_in%d" % s, 2 * nALL))
-        m = mark("t", g.tensor.matmul_mx(T.ps7[:, 0:TQ], T["kvc%d" % s][:, 512:KV], T["kvp%d" % s][:, 512:KV],
-                                         T["ac%d" % s][:], T["ap%d" % s][:], s == order[0], s == order[-1]))
+        return mark("t", g.tensor.matmul_mx(T.ps7[:, 0:TQ], T["vc%d" % s][:], T["vp%d" % s][:], T["ac%d" % s][:], T["ap%d" % s][:],
+                                            s == order[0], s == order[-1]))
+
+    value(r)
+    distances("f", KF, (0, 1), ("k0_in", 2 * nALL))
+    distances("f", KF, (2, 3), ("k1_in", 2 * nALL))
+    for b, q in ((0, "s"), (1, "s"), (2, "v"), (3, "v")):
+        window("f", b, q)
+    for b in B:
+        pick(3, "f", b, "off", 16 * b, lf)
+    scores(3, KF, OWN)
+    for b in range(3):
+        add(3, b)
+    made[far_s] = close(3, A(far_s))
+    for s in order[1:]:
+        m = value(s)
     after("s", m)
     m = mark("s", g.scalar.activation(T.ys[:], T.ps7[:, 0:TQ], COPY))
     after("s", m)

from concourse.bass import DstId, RemoteDMATransfer
from concourse.mybir import dt, AluOpType, ActivationFunctionType

NR, TQ = 6, 256
F8 = "float8_e4m3fn_x4"
RT, OWN, PRV, NXT = 0, 256, 512, 768
SCRATCH = {
    "kt": ("sbuf", [128, 2048], "bfloat16"),
    "xt": ("sbuf", [128, 1024], "bfloat16"),
    "rtt": ("sbuf", [128, 1024], "bfloat16"),
    "vt": ("sbuf", [128, 512], "bfloat16"),
    "mc": ("sbuf", [128, 1024], F8), "mp": ("sbuf", [128, 1024], "uint8"),
    "kco": ("sbuf", [128, 512], F8), "kpo": ("sbuf", [128, 512], "uint8"),
    "kcf": ("sbuf", [128, 512], F8), "kpf": ("sbuf", [128, 512], "uint8"),
    "kpi": ("sbuf", [128, 4], "int32"),
    "kfo": ("sbuf", [128, 4], "float32"), "kff": ("sbuf", [128, 4], "float32"),
    "qpi": ("sbuf", [128, 48], "int32"),
    "pwo": ("sbuf", [128, 1024], "float32"), "pwf": ("sbuf", [128, 1024], "float32"),
    "ys": ("sbuf", [128, 256], "float32"),
}
for _n, _w in (("o", 64), ("x", 128), ("f", 64)):
    SCRATCH["ot" + _n] = ("sbuf", [128, _w], "float32")
    SCRATCH["of" + _n] = ("sbuf", [128, _w], "uint16")
for _i in range(4):
    SCRATCH["gg%d" % _i] = ("sbuf", [128, 1024], "float32")
    SCRATCH["ht%d" % _i] = ("sbuf", [128, 1024], "bfloat16")
for _i in range(2):
    SCRATCH["oc%d" % _i] = ("sbuf", [128, TQ], F8)
    SCRATCH["op%d" % _i] = ("sbuf", [128, TQ], "uint8")
for _i in range(NR):
    SCRATCH["vc%d" % _i] = ("sbuf", [128, 128], F8)
    SCRATCH["vp%d" % _i] = ("sbuf", [128, 128], "uint8")
    SCRATCH["ac%d" % _i] = ("sbuf", [128, TQ], F8)
    SCRATCH["ap%d" % _i] = ("sbuf", [128, TQ], "uint8")
for _i in range(8):
    SCRATCH["ps%d" % _i] = ("psum", [128, 512], "float32")

SEMAPHORES = (["l_p", "l_q", "l_k0", "l_k1", "l_v", "l_r", "l_x", "vs", "ss", "ts", "sent", "stored",
               "q_in", "kf_in", "k0_in", "k1_in", "r_in", "xp_in", "xn_in"]
              + ["%s_in%d" % (n, i) for n in ("v", "a") for i in range(NR)])


def layout(T, topo):
    cores = list(T.cores)
    side = [[q for q in range(NR) if topo.chip(cores[q]) == topo.chip(cores[r])] for r in range(NR)]
    local, mirror, worker = [], [], []
    for r in range(NR):
        i = side[r].index(r)
        local.append(side[r][i:] + side[r][:i])
        mirror.append([q for q in range(NR) if q not in side[r]][i])
    for r in range(NR):
        idle = [c for c in topo.cores_of(cores[r]) if c not in cores and c not in worker]
        idle.sort(key=lambda c: (topo.die(c) != topo.die(cores[mirror[r]]), -c))
        worker.append(idle[0])
    return cores, local, mirror, worker


def rank_program(g, core, T, topo):
    cores, local, mirror, worker = layout(T, topo)
    rank = T.rank_of(core)
    if rank is None and core not in worker:
        return
    r, nxt, prv = local[rank if rank is not None else worker.index(core)]
    far_s = mirror[r]
    ADD, MAX, MIN, MULT, SUB = AluOpType.add, AluOpType.max, AluOpType.min, AluOpType.mult, AluOpType.subtract
    COPY = ActivationFunctionType.Copy
    eng = {"g": g, "v": g.vector, "s": g.scalar, "t": g.tensor}
    done, seen, sent = {"v": 0, "s": 0, "t": 0}, {}, [0]

    def after(q, *deps):
        for d in deps:
            sem = d[0] + "s" if d[0] in done else d[0]
            if seen.get((q, sem), 0) < d[1]:
                eng[q].wait_ge(T.sem[sem], d[1])
                seen[(q, sem)] = d[1]

    def mark(q, ins):
        ins.then_inc(T.sem[q + "s"], 1)
        done[q] += 1
        return (q, done[q])

    far = cores[mirror[0]] if topo.chip(core) == topo.chip(cores[0]) else cores[0]
    near = [c for c in topo.cores_of(core) if c != core][0]
    ALL = topo.engines(core, near)
    OFF = topo.engines(core, far)
    ON = [e for e in ALL if e not in OFF]
    nALL, nOFF, nON = len(ALL), len(OFF), len(ON)

    def ids(dsts):
        out = []
        for d in dsts:
            rid, pid = topo.addr(d)[:2]
            out.append(DstId(rid=rid, pnc=pid))
        return out

    def send(sems, src, *ways):
        if not isinstance(sems, list):
            sems = [sems] * len(ways)
        g.remote_dma_fused([RemoteDMATransfer(dst_ids=ids(ds), dma_engine_mask=sum(1 << e for e in es), remote_sem=T.sem[sem],
                                              srcs=[src], dsts=[to] * len(ds)) for sem, (es, ds, to) in zip(sems, ways)], local_sem=T.sem.sent)
        sent[0] += sum(len(es) for es, _, _ in ways)

    def codes(name, a, b):
        return T[name][:, a:b].bitcast(dt.uint8)

    def plane(name, a, b):
        return T[name][:, a:b]

    def ship(sems, src, a, n, *ways):
        for k, view in ((0, codes), (1, plane)):
            send(sems, view(src[k], a, a + n), *[(es, ds, view(to[k], ta, ta + n)) for es, ds, to, ta in ways])

    M, KO, KF = ("mc", "mp"), ("kco", "kpo"), ("kcf", "kpf")

    def V(s):
        return ("vc%d" % s, "vp%d" % s)

    def A(s):
        return ("ac%d" % s, "ap%d" % s)

    def quantise(to, a, b, src, *deps):
        after("v", *deps)
        return mark("v", g.vector.quantize_mx(T[to[0]][:, a:b], T[to[1]][:, a:b], src))

    def lists(n, kf, a, w, *deps):
        after("v", *deps)
        for b in range(4):
            m = mark("v", g.vector.tensor_scalar(T["ot" + n][:, w * b:w * b + w], T.qpi[:, a:a + w], T[kf][:, b:b + 1], 0.0, SUB, MAX))
        after("v", m)
        return mark("v", g.vector.tensor_scalar(T["of" + n][:], T["ot" + n][:], 255.0, None, MIN))

    banks = 7 if rank is not None else 8
    drained, turn = [()] * 8, [0]
    P, W, S, G, R = {}, {}, {}, {}, {}

    def product(K, b, a):
        k = turn[0] % banks
        turn[0] += 1
        after("t", *drained[k])
        return k, mark("t", g.tensor.matmul_mx(T["ps%d" % k][:, 0:TQ], T[K[0]][:, 128 * b:128 * b + 128], T[K[1]][:, 128 * b:128 * b + 128],
                                               T.mc[:, a:a + TQ], T.mp[:, a:a + TQ], True, True))

    def distances(n, K, bs, *deps):
        after("t", *deps)
        for b in bs:
            P[n, b] = product(K, b, RT)

    def scores(i, K, a, *deps):
        after("t", *deps)
        for b in range(4):
            S[i, b] = product(K, b, a)

    def window(n, b, q):
        k, m = P[n, b]
        d, p = T["pw" + n][:, TQ * b:TQ * b + TQ], T["ps%d" % k][:, 0:TQ]
        after(q, m)
        W[n, b] = mark(q, g.vector.tensor_copy(d, p) if q == "v" else g.scalar.activation(d, p, COPY))
        drained[k] = (W[n, b],)

    def pick(i, n, b, of, col, li):
        after("s", W[n, b], li)
        G[i, b] = mark("s", g.scalar.activation(T["gg%d" % i][:, TQ * b:TQ * b + TQ],
                                                T["pw" + n][:, TQ * b:TQ * b + TQ].indirect(T[of][:, col:col + 16]), COPY))

    def add(i, b):
        k, m = S[i, b]
        after("v", m, G[i, b])
        R[i, b] = mark("v", g.vector.tensor_tensor(T["ht%d" % i][:, b:4 * TQ:4], T["ps%d" % k][:, 0:TQ], T["gg%d" % i][:, TQ * b:TQ * b + TQ], ADD))
        drained[k] = (R[i, b],)

    def relu(i, b, step):
        after("v", *[R[i, c] for c in range(b, 4, step)])
        h = T["ht%d" % i][:, b:4 * TQ:step]
        R[i] = mark("v", g.vector.tensor_scalar(h, h, 0.0, 0.03125, MAX, MULT))

    def pack(i, to):
        return quantise(to, 0, TQ, T["ht%d" % i][:], R[i])

    def lace(i, j, to):
        add(j, 0)
        relu(i, 0, 1)
        add(j, 1)
        m = pack(i, to)
        add(j, 2)
        return m

    def close(i, to):
        relu(i, 0, 2)
        add(i, 3)
        relu(i, 1, 2)
        return pack(i, to)

    def farewell():
        after("g", ("v", done["v"]), ("s", done["s"]), ("t", done["t"]), ("sent", sent[0]))

    B = range(4)
    QIN = ("q_in", nON + nOFF)
    if rank is None:
        here, home = [cores[r]], [cores[q] for q in local[r]]
        KFIN = ("kf_in", nOFF)
        after("g", KFIN)
        send("kf_in", T.kff[:], (ALL, here, T.kff[:]))
        for i in range(2):
            after("g", ("k%d_in" % i, 2 * nOFF))
            ship("k%d_in" % i, KF, 256 * i, 256, (ALL, here, KF, 256 * i))
        after("g", ("v_in%d" % far_s, 2 * nOFF))
        ship("v_in%d" % far_s, V(far_s), 0, 128, (ALL, home, V(far_s), 0))

        li = lists("x", "kff", 16, 32, QIN, KFIN)
        distances("f", KF, (0, 1), ("r_in", 2 * nON), ("k0_in", 2 * nOFF))
        distances("f", KF, (2, 3), ("k1_in", 2 * nOFF))
        window("f", 0, "s")
        for b in (1, 2, 3):
            window("f", b, "v")
        for i in range(2):
            for b in B:
                pick(i, "f", b, "ofx", 32 * b + 16 * i, li)
        scores(0, KF, PRV, ("xp_in", 2 * nON))
        for b in B:
            add(0, b)
        scores(1, KF, NXT, ("xn_in", 2 * nOFF))
        made = [lace(0, 1, ("oc0", "op0")), close(1, ("oc1", "op1"))]
        for i, q in ((0, prv), (1, nxt)):
            after("g", made[i])
            ship("a_in%d" % far_s, ("oc%d" % i, "op%d" % i), 0, TQ, (ALL, [cores[q]], A(far_s), 0))
        farewell()
        return

    away, mine = [worker[far_s]], [worker[r]]
    to_nxt, to_prv = [cores[nxt], worker[nxt]], [cores[prv], worker[prv]]
    g.sync.dma_start(T.kpi[:], T.kp[:]).then_inc(T.sem.l_p, 16)
    for i in range(2):
        g.sync.dma_start(T.kt[:, 1024 * i:1024 * i + 1024], T.ky[:, 1024 * i:1024 * i + 1024]).then_inc(T.sem["l_k%d" % i], 16)
    g.sync.dma_start(T.rtt[:], T.rt[:]).then_inc(T.sem.l_r, 16)
    for k in range(8):
        g.scalar.dma_start(T.qpi[16 * k:16 * k + 16, 0:16], T.qp[:]).then_inc(T.sem.l_q, 16)
    g.scalar.dma_start(T.xt[:], T.qx[:]).then_inc(T.sem.l_x, 16)
    g.scalar.dma_start(T.vt[:], T.vv[:]).then_inc(T.sem.l_v, 16)
    LQ = ("l_q", 16 * 8)

    after("v", ("l_p", 16))
    mf = mark("v", g.vector.tensor_scalar(T.kfo[:], T.kpi[:], 128.0, None, SUB))
    after("g", mf)
    send("kf_in", T.kfo[:], (OFF, away, T.kff[:]))
    after("g", LQ)
    send("q_in", T.qpi[:, 0:16], (ON, to_nxt, T.qpi[:, 16:32]), (OFF, to_prv, T.qpi[:, 32:48]))
    for i in range(2):
        mk = quantise(KO, 256 * i, 256 * i + 256, T.kt[:, 1024 * i:1024 * i + 1024], ("l_k%d" % i, 16))
        after("g", mk)
        ship("k%d_in" % i, KO, 256 * i, 256, (OFF, away, KF, 256 * i))
    lo = lists("o", "kfo", 0, 16, mf, LQ)
    mr = quantise(M, RT, RT + TQ, T.rtt[:], ("l_r", 16))
    after("g", mr)
    ship("r_in", M, RT, TQ, (ON, mine, M, RT))
    mx = quantise(M, OWN, OWN + TQ, T.xt[:], ("l_x", 16))
    after("g", mx)
    ship(["xp_in", "xn_in"], M, OWN, TQ, (ON, to_nxt, M, PRV), (OFF, to_prv, M, NXT))

    distances("o", KO, B, mk, mr)
    for b, q in ((0, "s"), (1, "s"), (2, "v"), (3, "v")):
        window("o", b, q)
    scores(0, KO, OWN, mx)
    for b in B:
        pick(0, "o", b, "ofo", 16 * b, lo)
    add(0, 0)
    lx = lists("x", "kfo", 16, 32, QIN)
    for i in range(2):
        for b in B:
            pick(1 + i, "o", b, "ofx", 32 * b + 16 * i, lx)
    add(0, 1)
    mv = quantise(V(r), 0, 128, T.vt[:], ("l_v", 16))
    after("g", mv)
    ship("v_in%d" % r, V(r), 0, 128, (OFF, away, V(r), 0), (ON, [cores[nxt], cores[prv]], V(r), 0))
    add(0, 2)
    add(0, 3)
    scores(1, KO, PRV, ("xp_in", 2 * nON))
    made = {r: lace(0, 1, A(r))}
    lf = lists("f", "kff", 0, 16, ("kf_in", nALL))
    add(1, 3)
    scores(2, KO, NXT, ("xn_in", 2 * nOFF))
    m1 = lace(1, 2, ("oc0", "op0"))
    add(2, 3)
    relu(2, 0, 1)
    m2 = pack(2, ("oc1", "op1"))
    for i, q, m in ((0, prv, m1), (1, nxt, m2)):
        after("g", m)
        ship("a_in%d" % r, ("oc%d" % i, "op%d" % i), 0, TQ, (ALL, [cores[q]], A(r), 0))

    order = [r, nxt, prv, mirror[nxt], far_s, mirror[prv]]

    def value(s):
        after("t", mv if s == r else ("v_in%d" % s, 2 * (nON if s in (prv, nxt) else nALL)))
        after("t", made[s] if s in made else ("a_in%d" % s, 2 * nALL))
        return mark("t", g.tensor.matmul_mx(T.ps7[:, 0:TQ], T["vc%d" % s][:], T["vp%d" % s][:], T["ac%d" % s][:], T["ap%d" % s][:],
                                            s == order[0], s == order[-1]))

    value(r)
    distances("f", KF, (0, 1), ("k0_in", 2 * nALL))
    distances("f", KF, (2, 3), ("k1_in", 2 * nALL))
    for b, q in ((0, "s"), (1, "s"), (2, "v"), (3, "v")):
        window("f", b, q)
    for b in B:
        pick(3, "f", b, "off", 16 * b, lf)
    scores(3, KF, OWN)
    for b in range(3):
        add(3, b)
    made[far_s] = close(3, A(far_s))
    for s in order[1:]:
        m = value(s)
    after("s", m)
    m = mark("s", g.scalar.activation(T.ys[:], T.ps7[:, 0:TQ], COPY))
    after("s", m)
    g.scalar.dma_start(T.y[:], T.ys[:]).then_inc(T.sem.stored, 16)
    after("g", ("stored", 16))
    farewell()
